import numpy as np
import ml_dtypes


def mxq(x, axis, fmt="e4m3"):
    dtype, down = {"e4m3": (ml_dtypes.float8_e4m3fn, 7), "e5m2": (ml_dtypes.float8_e5m2, 14)}[fmt]
    v = np.moveaxis(np.asarray(x, np.float32).astype(ml_dtypes.bfloat16).astype(np.float64), axis, -1)
    blocks = v.reshape(v.shape[:-1] + (-1, 32))
    amax = np.abs(blocks).max(-1, keepdims=True)
    byte = np.maximum(np.where(amax > 0, np.frexp(amax)[1] - 1 + 127, 0) - down, 1)
    scale = np.exp2(byte - 127.0)
    codes = (blocks / scale).astype(np.float32).astype(dtype).astype(np.float64)
    return np.moveaxis((codes * scale).reshape(v.shape), -1, axis)


WIDE = False


def mx_kscale(k):
    if not WIDE:
        return np.ones(k)
    levels = np.array([10, -10, 5, -5, 0])
    if k % 512:
        return np.exp2(np.random.permutation(np.resize(levels, k // 32))).repeat(32)
    a = np.empty((k // 512, 16))
    for p in range(k // 512):
        a[p, :8] = np.random.permutation(np.resize(levels, 8))
        for g in range(8):
            far = levels[np.abs(levels - a[p, g]) >= 10]
            a[p, g + 8] = far[np.random.randint(len(far))]
    return np.exp2(a.ravel()).repeat(32)


def f64(x):
    return np.asarray(x).astype(np.float64)


def striped(idx):
    return np.tile(idx.reshape(-1, 16).T, (8, 1)).astype(np.uint16)


def unstriped(offs):
    return offs[:16].T.reshape(-1).astype(np.int64)


E2M1 = np.array([0.0, 0.5, 1.0, 1.5, 2.0, 3.0, 4.0, 6.0, -0.0, -0.5, -1.0, -1.5, -2.0, -3.0, -4.0, -6.0])


def pack_weight(w, fmt):
    k, n = w.shape
    w = f64(np.asarray(w, np.float32).astype(ml_dtypes.bfloat16)).reshape(k // 32, 32, n)
    amax = np.abs(w).max(1)
    if fmt == "e4m3":
        byte = np.frexp(amax)[1] - 1 + 127 - 7
    else:
        mant, ex = np.frexp(amax / 6.0)
        byte = np.where(mant > 0.5, ex, ex - 1) + 127
    byte = np.clip(np.where(amax > 0, byte, 1), 1, 254)
    scaled = (w * np.exp2(127.0 - byte)[:, None, :]).reshape(k, n).astype(np.float32)
    by_word = np.ascontiguousarray(scaled.reshape(k // 512, 128, 4, n).transpose(0, 1, 3, 2))
    if fmt == "e4m3":
        words = by_word.astype(ml_dtypes.float8_e4m3fn).view(np.uint8)
    else:
        c = by_word.astype(ml_dtypes.float4_e2m1fn).view(np.uint8) & 0xF
        words = (c[..., 0::2] | (c[..., 1::2] << 4)).reshape(k // 512, 128, 2 * n)
    return np.ascontiguousarray(words), np.ascontiguousarray(byte.astype(np.uint8).reshape(k // 512, 16, n))


def unpack_weight(words, scales, fmt):
    g, _, n = scales.shape
    words = np.ascontiguousarray(words).reshape(g, 128, n, -1)
    if fmt == "e4m3":
        vals = words.view(ml_dtypes.float8_e4m3fn).astype(np.float64)
    else:
        nib = np.empty((g, 128, n, 4), np.uint8)
        nib[..., 0::2] = words & 0xF
        nib[..., 1::2] = words >> 4
        vals = E2M1[nib]
    vals = vals * np.repeat(np.exp2(scales.astype(np.float64) - 127.0), 8, axis=1)[..., None]
    return vals.transpose(0, 1, 3, 2).reshape(g * 512, n)


def relu2(v):
    return np.maximum(v, 0.0) ** 2


K, T, E, C, H, N = 1536, 768, 4, 256, 512, 256
R = 2


def by_expert(wq, xq):
    return np.concatenate([wq[e].T @ xq[:, e * C:(e + 1) * C] for e in range(E)], axis=1)


def setup_inputs():
    n = np.random.standard_normal
    s = mx_kscale(K)[:, None]
    u = mx_kscale(H)
    slot_token = np.concatenate([r * (T // R) + np.random.permutation(T // R)[:C // R] for e in range(E) for r in range(R)])
    w1 = [pack_weight(m, "e2m1") for m in n((E, K, H)) / np.sqrt(K) / s[None] * u[None, None, :]]
    w2 = [pack_weight(m, "e2m1") for m in n((E, H, N)) / np.sqrt(H) / u[None, :, None] ** 2]
    return {
        "xT": (n((K, T)) * s).astype(np.float32),
        "w1_words": np.stack([m[0] for m in w1]),
        "w1_scales": np.stack([m[1] for m in w1]),
        "w2_words": np.stack([m[0] for m in w2]),
        "w2_scales": np.stack([m[1] for m in w2]),
        "offs": striped(slot_token),
    }


def reference(xT, w1_words, w1_scales, w2_words, w2_scales, offs):
    idx = unstriped(offs)
    w1 = np.stack([unpack_weight(w1_words[e], w1_scales[e], "e2m1") for e in range(E)])
    w2 = np.stack([unpack_weight(w2_words[e], w2_scales[e], "e2m1") for e in range(E)])
    xq = mxq(f64(xT)[:, idx], 0, "e4m3")
    h = relu2(by_expert(w1, xq))
    y = by_expert(w2, mxq(h, 0, "e4m3"))
    return y.reshape(N, E, R, C // R).transpose(0, 2, 1, 3).reshape(N, E * C)

@@ -1,0 +1,267 @@
+from contextlib import ExitStack
+
+import concourse.mybir as mybir
+from concourse.masks import make_identity
+
+F32 = mybir.dt.float32
+BF16 = mybir.dt.bfloat16
+I32 = mybir.dt.int32
+U32 = mybir.dt.uint32
+U16 = mybir.dt.uint16
+U8 = mybir.dt.uint8
+FP8 = mybir.dt.float8_e4m3fn_x4
+FP4 = mybir.dt.float4_e2m1fn_x4
+RELU = mybir.ActivationFunctionType.Relu
+SQUARE = mybir.ActivationFunctionType.Square
+MULT = mybir.AluOpType.mult
+MAX = mybir.AluOpType.max
+
+K, T, E, C, H, N, R = 1536, 768, 4, 256, 512, 256, 2
+P = 128
+S = K // 512
+TR = T // R
+B = C // R
+FLOPS = 2 * E * C * (K * H + H * N)
+
+
+def tile_moe_eps_mlp_relu2_kernel(tc, xT, w1_words, w1_scales, w2_words, w2_scales, offs, out):
+    nc = tc.nc
+    with ExitStack() as ctx:
+        keep = ctx.enter_context(tc.tile_pool(name="keep", bufs=1))
+        ring = ctx.enter_context(tc.tile_pool(name="ring", bufs=4))
+        acc_pool = ctx.enter_context(tc.psum_pool(name="acc_pool", bufs=4))
+        tr_pool = ctx.enter_context(tc.psum_pool(name="tr_pool", bufs=2))
+        y_pool = ctx.enter_context(tc.psum_pool(name="y_pool", bufs=1))
+
+        offsets = keep.tile([P, E * C // 16], U16, name="offsets")
+        nc.sync.dma_start(offsets[:], offs)
+
+        xf = [keep.tile([P, 4, T], F32, name=f"xf{s}") for s in range(S)]
+        xb = [keep.tile([P, T, 4], BF16, name=f"xb{s}", align_bytes=64) for s in range(S)]
+        w1t = [keep.tile([P, S, 2 * H], U8, name=f"w1t{e}", align_bytes=64) for e in range(E)]
+        w1s = keep.tile([P, E, S, H], U8, name="w1s", align_bytes=64)
+        w2t = keep.tile([P, E, 2 * N], U8, name="w2t", align_bytes=64)
+        w2s = keep.tile([P, E, N], U8, name="w2s", align_bytes=64)
+        codes = [keep.tile([P, T], U32, name=f"codes{s}", align_bytes=64) for s in range(S)]
+        tsc01 = keep.tile([P, T], U8, name="tsc01", align_bytes=64)
+        tsc2 = keep.tile([P, T], U8, name="tsc2", align_bytes=64)
+        gw = [keep.tile([P, E * C], U32, name=f"gw{s}", align_bytes=64) for s in range(S)]
+        gb01 = keep.tile([P, E * C], U8, name="gb01", align_bytes=64)
+        gb1 = keep.tile([P, E * C], U8, name="gb1", align_bytes=64)
+        gb2 = keep.tile([P, E * C], U8, name="gb2", align_bytes=64)
+        ident = keep.tile([P, P], F32, name="ident")
+        warm = keep.tile([P, 1], F32, name="warm")
+
+        def load_x(s, a, b):
+            src = xT[512 * s : 512 * (s + 1), a:b].rearrange("(p j) w -> p j w", j=4)
+            nc.sync.dma_start(xf[s][:, :, a:b], src)
+
+        def load_w1(e):
+            nc.sync.dma_start(w1t[e][:].bitcast(I32), w1_words[e].rearrange("s p w -> p s w").bitcast(I32))
+
+        def load_w1s():
+            for q in range(4):
+                nc.sync.dma_start(
+                    w1s[32 * q : 32 * q + 4, :, :, :].rearrange("p e s n -> p (e s) n").bitcast(I32),
+                    w1_scales[:, :, 4 * q : 4 * q + 4, :].rearrange("e s q n -> q (e s) n").bitcast(I32),
+                )
+
+        def load_w2():
+            for q in range(4):
+                nc.sync.dma_start(
+                    w2s[32 * q : 32 * q + 4, :, :].bitcast(I32),
+                    w2_scales[:, 0, 4 * q : 4 * q + 4, :].rearrange("e q n -> q e n").bitcast(I32),
+                )
+            nc.sync.dma_start(w2t[:].bitcast(I32), w2_words[:, 0].rearrange("e p w -> p e w").bitcast(I32))
+
+        nc.gpsimd.memset(warm[:], 0.0)
+        nc.gpsimd.memset(tsc01[:], 0)
+        nc.gpsimd.memset(w1s[:].rearrange("p e s n -> p (e s n)").bitcast(I32), 0)
+        nc.gpsimd.memset(gb1[:].bitcast(I32), 0)
+        nc.gpsimd.memset(tsc2[:], 0)
+        nc.gpsimd.memset(w2s[:].rearrange("p e n -> p (e n)").bitcast(I32), 0)
+        make_identity(nc, ident[:])
+        nc.scalar.activation(warm[:], warm[:], RELU)
+
+        load_x(0, 0, 512)
+        load_x(0, 512, 768)
+        load_x(1, 0, 768)
+        load_w1s()
+        load_w1(0)
+        load_x(2, 0, 768)
+        load_w1(1)
+        load_w2()
+        load_w1(2)
+        load_w1(3)
+
+        def cast(s, eng, a, b):
+            dst = xb[s][:, a:b, :]
+            src = xf[s][:, :, a:b].rearrange("p j w -> p w j")
+            if eng == "v":
+                nc.vector.tensor_copy(dst, src)
+            else:
+                nc.scalar.copy(dst, src)
+
+        def quant(s, a, b):
+            plane, k = ((tsc01, 0), (tsc01, 4), (tsc2, 0))[s]
+            nc.vector.quantize_mx(
+                out=codes[s][:, a:b].bitcast(FP8),
+                scales=plane[k:P, a:b],
+                in_=xb[s][:, a:b, :].rearrange("p w j -> p (w j)"),
+            )
+
+        def gather(dst, src, a, b):
+            nc.vector.tensor_copy(dst[:, a:b], src[:].indirect(offsets[:, a // 16 : b // 16]))
+
+        def shift(a, b):
+            for q in range(4):
+                nc.sync.dma_start(gb1[32 * q : 32 * q + 4, a:b].bitcast(I32), gb01[32 * q + 4 : 32 * q + 8, a:b].bitcast(I32))
+
+        acc = {}
+
+        def layer1(b, s):
+            if s == 0:
+                acc[b] = acc_pool.tile([P, H], F32, name="acc")
+            cols = slice(b * B, (b + 1) * B)
+            e = b // R
+            nc.tensor.matmul_mx(
+                out=acc[b][:],
+                lhsT=gw[s][:, cols].bitcast(FP8),
+                lhsT_scale=(gb01, gb1, gb2)[s][:, cols],
+                rhs=w1t[e][:, s, :].bitcast(FP4),
+                rhs_scale=w1s[:, e, s, :],
+                start=(s == 0),
+                stop=(s == S - 1),
+            )
+
+        relu = {}
+        h = {}
+        y = {}
+
+        def relu_of(b, cuts):
+            relu[b] = ring.tile([P, H], F32, name="relu")
+            for eng, lo, hi in cuts:
+                if eng == "s":
+                    nc.scalar.activation(relu[b][:, lo:hi], acc[b][:, lo:hi], RELU)
+                else:
+                    nc.vector.tensor_scalar(relu[b][:, lo:hi], acc[b][:, lo:hi], 0.0, None, MAX)
+
+        def square_of(b, cuts):
+            h[b] = ring.tile([P, 2, P, 2], BF16, name="h", align_bytes=64)
+            rv = relu[b][:].rearrange("c (p u d) -> c u p d", u=2, d=2)
+            for eng, lo, hi in cuts:
+                o = h[b][:, :, lo:hi, :]
+                i = rv[:, :, lo:hi, :]
+                if eng == "g":
+                    nc.gpsimd.tensor_tensor(o, i, i, MULT)
+                elif eng == "v":
+                    nc.vector.tensor_tensor(o, i, i, MULT)
+                else:
+                    nc.scalar.activation(o, i, SQUARE)
+
+        def second(b, ev):
+            e, m = b // R, b % R
+            tr = tr_pool.tile([P, 2, P], F32, name="tr")
+            hw = h[b][:].rearrange("c u p d -> c (u p d)").bitcast(F32)
+            for u in range(2):
+                nc.tensor.transpose(tr[:, u, :], hw[:, P * u : P * (u + 1)], ident[:])
+            hq = ring.tile([P, B, 4], BF16, name="hq", align_bytes=64)
+            hqw = hq[:].rearrange("p c d -> p (c d)")
+            dst = hqw.bitcast(F32).rearrange("p (c u) -> p c u", u=2)
+            src = tr[:].rearrange("p u c -> p c u")
+            if ev == "s":
+                nc.scalar.copy(dst, src)
+            else:
+                nc.vector.tensor_copy(dst, src)
+            hc = ring.tile([P, B], U32, name="hc", align_bytes=64)
+            hs = ring.tile([P, B], U8, name="hs", align_bytes=64)
+            nc.vector.quantize_mx(out=hc[:].bitcast(FP8), scales=hs[:], in_=hqw)
+            if (b // 4, 0) not in y:
+                for n in range(2):
+                    y[b // 4, n] = y_pool.tile([P, 4 * B], F32, name=f"y{n}")
+            at = m * 2 * B + (e % 2) * B
+            for n in range(2):
+                nc.tensor.matmul_mx(
+                    out=y[b // 4, n][:, at : at + B],
+                    lhsT=w2t[:, e, 256 * n : 256 * (n + 1)].bitcast(FP4),
+                    lhsT_scale=w2s[:, e, P * n : P * (n + 1)],
+                    rhs=hc[:].bitcast(FP8),
+                    rhs_scale=hs[:],
+                    start=True,
+                    stop=True,
+                )
+
+        def store(g, engs):
+            for n in range(2):
+                o = ring.tile([P, 4 * B], F32, name=f"o{n}")
+                if engs[n] == "v":
+                    nc.vector.tensor_copy(o[:], y[g, n][:])
+                else:
+                    nc.scalar.copy(o[:], y[g, n][:])
+                dst = out[P * n : P * (n + 1), :].rearrange("n (m x) -> n m x", m=2)[:, :, 2 * B * g : 2 * B * (g + 1)]
+                nc.sync.dma_start(dst, o[:].rearrange("p (m x) -> p m x", m=2))
+
+        FULL_S = (("s", 0, H),)
+        FULL_V = (("v", 0, H),)
+        cast(0, "v", 0, 256)
+        cast(0, "s", 256, 512)
+        quant(0, 0, 512)
+        cast(0, "v", 512, 640)
+        cast(0, "s", 640, 768)
+        quant(0, 512, 768)
+        gather(gw[0], codes[0], 0, 512)
+        gather(gw[0], codes[0], 512, 1024)
+        cast(1, "v", 0, 512)
+        cast(1, "s", 512, 768)
+        quant(1, 0, 512)
+        quant(1, 512, 768)
+        gather(gb01, tsc01, 0, 512)
+        shift(0, 512)
+        gather(gw[1], codes[1], 0, 512)
+        cast(2, "s", 0, 256)
+        cast(2, "s", 256, 512)
+        cast(2, "s", 512, 768)
+        for b in range(4):
+            layer1(b, 0)
+        for b in range(4):
+            layer1(b, 1)
+        quant(2, 0, 512)
+        quant(2, 512, 768)
+        gather(gb2, tsc2, 0, 512)
+        gather(gw[2], codes[2], 0, 512)
+        for b in range(4):
+            layer1(b, 2)
+            relu_of(b, FULL_S)
+        square_of(0, (("g", 0, P),))
+        square_of(1, (("g", 0, P),))
+        square_of(2, (("s", 0, P),))
+        square_of(3, (("s", 0, P),))
+        gather(gb01, tsc01, 512, 1024)
+        shift(512, 1024)
+        gather(gw[1], codes[1], 512, 1024)
+        for b in range(4, 8):
+            layer1(b, 0)
+        second(0, "s")
+        gather(gb2, tsc2, 512, 1024)
+        second(2, "s")
+        second(1, "s")
+        for b in range(4, 8):
+            layer1(b, 1)
+        gather(gw[2], codes[2], 512, 1024)
+        second(3, "s")
+        for b in range(4, 8):
+            layer1(b, 2)
+        relu_of(4, FULL_V)
+        relu_of(5, FULL_S)
+        relu_of(6, FULL_V)
+        relu_of(7, FULL_S)
+        square_of(4, (("g", 0, P),))
+        square_of(6, (("v", 0, P),))
+        square_of(5, (("s", 0, P),))
+        square_of(7, (("v", 0, P),))
+        store(0, "ss")
+        second(6, "s")
+        second(4, "v")
+        second(5, "s")
+        second(7, "v")
+        store(1, "vs")

@@ -66,12 +66,14 @@ def tile_moe_eps_mlp_relu2_kernel(tc, xT, w1_words, w1_scales, w2_words, w2_scal
                     w1_scales[:, :, 4 * q : 4 * q + 4, :].rearrange("e s q n -> q (e s) n").bitcast(I32),
                 )
 
-        def load_w2():
+        def load_w2s():
             for q in range(4):
                 nc.sync.dma_start(
                     w2s[32 * q : 32 * q + 4, :, :].bitcast(I32),
                     w2_scales[:, 0, 4 * q : 4 * q + 4, :].rearrange("e q n -> q e n").bitcast(I32),
                 )
+
+        def load_w2():
             nc.sync.dma_start(w2t[:].bitcast(I32), w2_words[:, 0].rearrange("e p w -> p e w").bitcast(I32))
 
         nc.gpsimd.memset(warm[:], 0.0)
@@ -86,17 +88,18 @@ def tile_moe_eps_mlp_relu2_kernel(tc, xT, w1_words, w1_scales, w2_words, w2_scal
         load_x(0, 0, 512)
         load_x(0, 512, 768)
         load_x(1, 0, 768)
-        load_w1s()
-        load_w1(0)
         load_x(2, 0, 768)
+        load_w1s()
+        load_w2s()
+        load_w1(0)
         load_w1(1)
         load_w2()
         load_w1(2)
         load_w1(3)
 
         def cast(s, eng, a, b):
-            dst = xb[s][:, a:b, :]
-            src = xf[s][:, :, a:b].rearrange("p j w -> p w j")
+            dst = xb[s][:, a:b, :].rearrange("p (c i) j -> p c j i", i=4)
+            src = xf[s][:, :, a:b].rearrange("p j (c i) -> p c j i", i=4)
             if eng == "v":
                 nc.vector.tensor_copy(dst, src)
             else:
@@ -203,6 +206,7 @@ def tile_moe_eps_mlp_relu2_kernel(tc, xT, w1_words, w1_scales, w2_words, w2_scal
 
         FULL_S = (("s", 0, H),)
         FULL_V = (("v", 0, H),)
+        SQ = {"s": (("s", 0, P),), "v": (("v", 0, P),), "g": (("g", 0, P),)}
         cast(0, "v", 0, 256)
         cast(0, "s", 256, 512)
         quant(0, 0, 512)
@@ -211,16 +215,19 @@ def tile_moe_eps_mlp_relu2_kernel(tc, xT, w1_words, w1_scales, w2_words, w2_scal
         quant(0, 512, 768)
         gather(gw[0], codes[0], 0, 512)
         gather(gw[0], codes[0], 512, 1024)
-        cast(1, "v", 0, 512)
-        cast(1, "s", 512, 768)
+        cast(1, "v", 0, 256)
+        cast(1, "s", 256, 512)
         quant(1, 0, 512)
+        cast(1, "v", 512, 640)
+        cast(1, "s", 640, 768)
         quant(1, 512, 768)
         gather(gb01, tsc01, 0, 512)
         shift(0, 512)
-        gather(gw[1], codes[1], 0, 512)
-        cast(2, "s", 0, 256)
+        cast(2, "v", 0, 256)
         cast(2, "s", 256, 512)
-        cast(2, "s", 512, 768)
+        cast(2, "s", 512, 640)
+        cast(2, "v", 640, 768)
+        gather(gw[1], codes[1], 0, 512)
         for b in range(4):
             layer1(b, 0)
         for b in range(4):
@@ -231,37 +238,40 @@ def tile_moe_eps_mlp_relu2_kernel(tc, xT, w1_words, w1_scales, w2_words, w2_scal
         gather(gw[2], codes[2], 0, 512)
         for b in range(4):
             layer1(b, 2)
-            relu_of(b, FULL_S)
-        square_of(0, (("g", 0, P),))
-        square_of(1, (("g", 0, P),))
-        square_of(2, (("s", 0, P),))
-        square_of(3, (("s", 0, P),))
         gather(gb01, tsc01, 512, 1024)
         shift(512, 1024)
+        relu_of(0, FULL_S)
+        relu_of(1, FULL_S)
+        square_of(0, SQ["s"])
         gather(gw[1], codes[1], 512, 1024)
         for b in range(4, 8):
             layer1(b, 0)
-        second(0, "s")
+        relu_of(2, FULL_S)
+        square_of(1, SQ["s"])
         gather(gb2, tsc2, 512, 1024)
-        second(2, "s")
+        second(0, "s")
+        relu_of(3, FULL_S)
+        square_of(2, SQ["s"])
         second(1, "s")
         for b in range(4, 8):
             layer1(b, 1)
         gather(gw[2], codes[2], 512, 1024)
-        second(3, "s")
         for b in range(4, 8):
             layer1(b, 2)
-        relu_of(4, FULL_V)
-        relu_of(5, FULL_S)
-        relu_of(6, FULL_V)
-        relu_of(7, FULL_S)
-        square_of(4, (("g", 0, P),))
-        square_of(6, (("v", 0, P),))
-        square_of(5, (("s", 0, P),))
-        square_of(7, (("v", 0, P),))
-        store(0, "ss")
-        second(6, "s")
-        second(4, "v")
-        second(5, "s")
+        square_of(3, SQ["v"])
+        relu_of(4, FULL_S)
+        second(2, "s")
+        relu_of(5, FULL_V)
+        square_of(4, SQ["s"])
+        square_of(5, SQ["v"])
+        second(3, "v")
+        relu_of(6, FULL_S)
+        relu_of(7, FULL_V)
+        square_of(7, SQ["v"])
+        square_of(6, SQ["s"])
+        second(4, "s")
+        second(5, "v")
+        store(0, "sv")
         second(7, "v")
+        second(6, "s")
         store(1, "vs")

@@ -9,269 +9,300 @@ I32 = mybir.dt.int32
 U32 = mybir.dt.uint32
 U16 = mybir.dt.uint16
 U8 = mybir.dt.uint8
-FP8 = mybir.dt.float8_e4m3fn_x4
-FP4 = mybir.dt.float4_e2m1fn_x4
+E4M3 = mybir.dt.float8_e4m3fn_x4
+E2M1 = mybir.dt.float4_e2m1fn_x4
 RELU = mybir.ActivationFunctionType.Relu
 SQUARE = mybir.ActivationFunctionType.Square
 MULT = mybir.AluOpType.mult
 MAX = mybir.AluOpType.max
 
-K, T, E, C, H, N, R = 1536, 768, 4, 256, 512, 256, 2
+K, T, E, C, H, N = 1536, 768, 4, 256, 512, 256
+R = 2
 P = 128
 S = K // 512
-TR = T // R
-B = C // R
-FLOPS = 2 * E * C * (K * H + H * N)
+SLOTS = E * C
+FLOPS = 2 * SLOTS * (K * H + H * N)
+
+WIDE = 1536
+
+VECTOR, SCALAR = "vector", "scalar"
 
 
 def tile_moe_eps_mlp_relu2_kernel(tc, xT, w1_words, w1_scales, w2_words, w2_scales, offs, out):
     nc = tc.nc
     with ExitStack() as ctx:
         keep = ctx.enter_context(tc.tile_pool(name="keep", bufs=1))
-        ring = ctx.enter_context(tc.tile_pool(name="ring", bufs=4))
+        ring = ctx.enter_context(tc.tile_pool(name="ring", bufs=8))
         acc_pool = ctx.enter_context(tc.psum_pool(name="acc_pool", bufs=4))
-        tr_pool = ctx.enter_context(tc.psum_pool(name="tr_pool", bufs=2))
+        turn_pool = ctx.enter_context(tc.psum_pool(name="turn_pool", bufs=2))
         y_pool = ctx.enter_context(tc.psum_pool(name="y_pool", bufs=1))
 
-        offsets = keep.tile([P, E * C // 16], U16, name="offsets")
+        offsets = keep.tile([P, SLOTS // 16], U16, name="offsets")
         nc.sync.dma_start(offsets[:], offs)
 
-        xf = [keep.tile([P, 4, T], F32, name=f"xf{s}") for s in range(S)]
-        xb = [keep.tile([P, T, 4], BF16, name=f"xb{s}", align_bytes=64) for s in range(S)]
-        w1t = [keep.tile([P, S, 2 * H], U8, name=f"w1t{e}", align_bytes=64) for e in range(E)]
-        w1s = keep.tile([P, E, S, H], U8, name="w1s", align_bytes=64)
-        w2t = keep.tile([P, E, 2 * N], U8, name="w2t", align_bytes=64)
-        w2s = keep.tile([P, E, N], U8, name="w2s", align_bytes=64)
-        codes = [keep.tile([P, T], U32, name=f"codes{s}", align_bytes=64) for s in range(S)]
-        tsc01 = keep.tile([P, T], U8, name="tsc01", align_bytes=64)
-        tsc2 = keep.tile([P, T], U8, name="tsc2", align_bytes=64)
-        gw = [keep.tile([P, E * C], U32, name=f"gw{s}", align_bytes=64) for s in range(S)]
-        gb01 = keep.tile([P, E * C], U8, name="gb01", align_bytes=64)
-        gb1 = keep.tile([P, E * C], U8, name="gb1", align_bytes=64)
-        gb2 = keep.tile([P, E * C], U8, name="gb2", align_bytes=64)
+        x_raw = [keep.tile([P, 4, T], F32, name=f"x_raw{s}") for s in range(S)]
+        x_grouped = [keep.tile([P, T, 4], BF16, name=f"x_grouped{s}", align_bytes=64) for s in range(S)]
+        w1_codes = [keep.tile([P, S, 2 * H], U8, name=f"w1_codes{e}", align_bytes=64) for e in range(E)]
+        w1_bytes = keep.tile([P, E, S, H], U8, name="w1_bytes", align_bytes=64)
+        w2_codes = keep.tile([P, E, 2 * N], U8, name="w2_codes", align_bytes=64)
+        w2_bytes = keep.tile([P, E, N], U8, name="w2_bytes", align_bytes=64)
+
+        token_words = [keep.tile([P, (WIDE, WIDE, T)[s]], U32, name=f"token_words{s}", align_bytes=64) for s in range(S)]
+        token_bytes01 = keep.tile([P, WIDE], U8, name="token_bytes01", align_bytes=64)
+        token_bytes2 = keep.tile([P, T], U8, name="token_bytes2", align_bytes=64)
+
+        slot_words = [keep.tile([P, SLOTS], U32, name=f"slot_words{s}", align_bytes=64) for s in range(S)]
+        slot_bytes01 = keep.tile([P, SLOTS], U8, name="slot_bytes01", align_bytes=64)
+        slot_bytes1 = keep.tile([P, SLOTS], U8, name="slot_bytes1", align_bytes=64)
+        slot_bytes2 = keep.tile([P, SLOTS], U8, name="slot_bytes2", align_bytes=64)
+        slot_planes = (slot_bytes01, slot_bytes1, slot_bytes2)
+
         ident = keep.tile([P, P], F32, name="ident")
-        warm = keep.tile([P, 1], F32, name="warm")
+        first = keep.tile([P, 1], F32, name="first")
 
-        def load_x(s, a, b):
-            src = xT[512 * s : 512 * (s + 1), a:b].rearrange("(p j) w -> p j w", j=4)
-            nc.sync.dma_start(xf[s][:, :, a:b], src)
+        nc.gpsimd.memset(first[:], 0.0)
+        nc.vector.memset(token_bytes01[:].bitcast(I32), 0)
+        nc.vector.memset(token_words[0][:, T:WIDE].bitcast(I32), 0)
+        nc.vector.memset(token_words[1][:, T:WIDE].bitcast(I32), 0)
+        nc.vector.memset(token_bytes2[:].bitcast(I32), 0)
+        nc.gpsimd.memset(w1_bytes[:].rearrange("p e s n -> p (e s n)").bitcast(I32), 0)
+        nc.gpsimd.memset(w2_bytes[:].rearrange("p e n -> p (e n)").bitcast(I32), 0)
+        nc.gpsimd.memset(slot_bytes1[:].bitcast(I32), 0)
+        make_identity(nc, ident[:])
+        nc.scalar.activation(first[:], first[:], RELU)
 
-        def load_w1(e):
-            nc.sync.dma_start(w1t[e][:].bitcast(I32), w1_words[e].rearrange("s p w -> p s w").bitcast(I32))
+        def load_tokens(s, a, b):
+            rows = xT[512 * s : 512 * (s + 1), a:b].rearrange("(p j) w -> p j w", j=4)
+            nc.sync.dma_start(x_raw[s][:, :, a:b], rows)
 
-        def load_w1s():
+        def load_weight_scales():
             for q in range(4):
                 nc.sync.dma_start(
-                    w1s[32 * q : 32 * q + 4, :, :, :].rearrange("p e s n -> p (e s) n").bitcast(I32),
+                    w1_bytes[32 * q : 32 * q + 4, :, :, :].rearrange("p e s n -> p (e s) n").bitcast(I32),
                     w1_scales[:, :, 4 * q : 4 * q + 4, :].rearrange("e s q n -> q (e s) n").bitcast(I32),
                 )
-
-        def load_w2s():
             for q in range(4):
                 nc.sync.dma_start(
-                    w2s[32 * q : 32 * q + 4, :, :].bitcast(I32),
+                    w2_bytes[32 * q : 32 * q + 4, :, :].bitcast(I32),
                     w2_scales[:, 0, 4 * q : 4 * q + 4, :].rearrange("e q n -> q e n").bitcast(I32),
                 )
 
+        def load_w1(e):
+            nc.sync.dma_start(w1_codes[e][:].bitcast(I32), w1_words[e].rearrange("s p w -> p s w").bitcast(I32))
+
         def load_w2():
-            nc.sync.dma_start(w2t[:].bitcast(I32), w2_words[:, 0].rearrange("e p w -> p e w").bitcast(I32))
+            nc.sync.dma_start(w2_codes[:].bitcast(I32), w2_words[:, 0].rearrange("e p w -> p e w").bitcast(I32))
 
-        nc.gpsimd.memset(warm[:], 0.0)
-        nc.gpsimd.memset(tsc01[:], 0)
-        nc.gpsimd.memset(w1s[:].rearrange("p e s n -> p (e s n)").bitcast(I32), 0)
-        nc.gpsimd.memset(gb1[:].bitcast(I32), 0)
-        nc.gpsimd.memset(tsc2[:], 0)
-        nc.gpsimd.memset(w2s[:].rearrange("p e n -> p (e n)").bitcast(I32), 0)
-        make_identity(nc, ident[:])
-        nc.scalar.activation(warm[:], warm[:], RELU)
-
-        load_x(0, 0, 512)
-        load_x(0, 512, 768)
-        load_x(1, 0, 768)
-        load_x(2, 0, 768)
-        load_w1s()
-        load_w2s()
-        load_w1(0)
-        load_w1(1)
-        load_w2()
-        load_w1(2)
-        load_w1(3)
-
-        def cast(s, eng, a, b):
-            dst = xb[s][:, a:b, :].rearrange("p (c i) j -> p c j i", i=4)
-            src = xf[s][:, :, a:b].rearrange("p j (c i) -> p c j i", i=4)
-            if eng == "v":
+        def cast(s, engine, a, b):
+            dst = x_grouped[s][:, a:b, :].rearrange("p (c i) j -> p c j i", i=4)
+            src = x_raw[s][:, :, a:b].rearrange("p j (c i) -> p c j i", i=4)
+            if engine == VECTOR:
                 nc.vector.tensor_copy(dst, src)
             else:
                 nc.scalar.copy(dst, src)
 
-        def quant(s, a, b):
-            plane, k = ((tsc01, 0), (tsc01, 4), (tsc2, 0))[s]
-            nc.vector.quantize_mx(
-                out=codes[s][:, a:b].bitcast(FP8),
-                scales=plane[k:P, a:b],
-                in_=xb[s][:, a:b, :].rearrange("p w j -> p (w j)"),
-            )
+        def quantise_tokens(s):
+            plane, row = ((token_bytes01, 0), (token_bytes01, 4), (token_bytes2, 0))[s]
+            for a, b in ((0, 512), (512, T)):
+                nc.vector.quantize_mx(
+                    out=token_words[s][:, a:b].bitcast(E4M3),
+                    scales=plane[row:P, a:b],
+                    in_=x_grouped[s][:, a:b, :].rearrange("p w j -> p (w j)"),
+                )
 
-        def gather(dst, src, a, b):
-            nc.vector.tensor_copy(dst[:, a:b], src[:].indirect(offsets[:, a // 16 : b // 16]))
+        def gather(slots, tokens, a, b):
+            nc.vector.tensor_copy(slots[:, a:b], tokens[:].indirect(offsets[:, a // 16 : b // 16]))
 
-        def shift(a, b):
+        def move_bytes1():
             for q in range(4):
-                nc.sync.dma_start(gb1[32 * q : 32 * q + 4, a:b].bitcast(I32), gb01[32 * q + 4 : 32 * q + 8, a:b].bitcast(I32))
+                nc.sync.dma_start(
+                    slot_bytes1[32 * q : 32 * q + 4, :].bitcast(I32),
+                    slot_bytes01[32 * q + 4 : 32 * q + 8, :].bitcast(I32),
+                )
 
         acc = {}
 
         def layer1(b, s):
             if s == 0:
                 acc[b] = acc_pool.tile([P, H], F32, name="acc")
-            cols = slice(b * B, (b + 1) * B)
-            e = b // R
+            slots = slice(P * b, P * (b + 1))
             nc.tensor.matmul_mx(
                 out=acc[b][:],
-                lhsT=gw[s][:, cols].bitcast(FP8),
-                lhsT_scale=(gb01, gb1, gb2)[s][:, cols],
-                rhs=w1t[e][:, s, :].bitcast(FP4),
-                rhs_scale=w1s[:, e, s, :],
+                lhsT=slot_words[s][:, slots].bitcast(E4M3),
+                lhsT_scale=slot_planes[s][:, slots],
+                rhs=w1_codes[b // R][:, s, :].bitcast(E2M1),
+                rhs_scale=w1_bytes[:, b // R, s, :],
                 start=(s == 0),
                 stop=(s == S - 1),
             )
 
-        relu = {}
+        rectified = {}
         h = {}
+        h_grouped = {}
+        h_words = {}
+        h_bytes = {}
+        turned = {}
         y = {}
 
-        def relu_of(b, cuts):
-            relu[b] = ring.tile([P, H], F32, name="relu")
-            for eng, lo, hi in cuts:
-                if eng == "s":
-                    nc.scalar.activation(relu[b][:, lo:hi], acc[b][:, lo:hi], RELU)
-                else:
-                    nc.vector.tensor_scalar(relu[b][:, lo:hi], acc[b][:, lo:hi], 0.0, None, MAX)
+        def rectify(b, engine):
+            rectified[b] = ring.tile([P, H], F32, name="rectified")
+            if engine == SCALAR:
+                nc.scalar.activation(rectified[b][:], acc[b][:], RELU)
+            else:
+                nc.vector.tensor_scalar(rectified[b][:], acc[b][:], 0.0, None, MAX)
 
-        def square_of(b, cuts):
+        def square(b, engine):
             h[b] = ring.tile([P, 2, P, 2], BF16, name="h", align_bytes=64)
-            rv = relu[b][:].rearrange("c (p u d) -> c u p d", u=2, d=2)
-            for eng, lo, hi in cuts:
-                o = h[b][:, :, lo:hi, :]
-                i = rv[:, :, lo:hi, :]
-                if eng == "g":
-                    nc.gpsimd.tensor_tensor(o, i, i, MULT)
-                elif eng == "v":
-                    nc.vector.tensor_tensor(o, i, i, MULT)
-                else:
-                    nc.scalar.activation(o, i, SQUARE)
+            v = rectified[b][:].rearrange("c (p u d) -> c u p d", u=2, d=2)
+            if engine == SCALAR:
+                nc.scalar.activation(h[b][:], v, SQUARE)
+            else:
+                nc.vector.tensor_tensor(h[b][:], v, v, MULT)
 
-        def second(b, ev):
-            e, m = b // R, b % R
-            tr = tr_pool.tile([P, 2, P], F32, name="tr")
-            hw = h[b][:].rearrange("c u p d -> c (u p d)").bitcast(F32)
-            for u in range(2):
-                nc.tensor.transpose(tr[:, u, :], hw[:, P * u : P * (u + 1)], ident[:])
-            hq = ring.tile([P, B, 4], BF16, name="hq", align_bytes=64)
-            hqw = hq[:].rearrange("p c d -> p (c d)")
-            dst = hqw.bitcast(F32).rearrange("p (c u) -> p c u", u=2)
-            src = tr[:].rearrange("p u c -> p c u")
-            if ev == "s":
+        def turn(*blocks):
+            tile = turn_pool.tile([P, len(blocks), 2, P], F32, name="turned")
+            for k, b in enumerate(blocks):
+                words = h[b][:].rearrange("c u p d -> c (u p d)").bitcast(F32)
+                for u in range(2):
+                    nc.tensor.transpose(tile[:, k, u, :], words[:, P * u : P * (u + 1)], ident[:])
+            turned[blocks] = tile
+
+        def group(engine, *blocks):
+            e = blocks[0] // R
+            if e not in h_grouped:
+                h_grouped[e] = ring.tile([P, C, 4], BF16, name="h_grouped", align_bytes=64)
+            at = P * (blocks[0] % R)
+            words = h_grouped[e][:, at : at + P * len(blocks), :].rearrange("p c d -> p (c d)").bitcast(F32)
+            if len(blocks) == 1:
+                dst = words.rearrange("p (c u) -> p c u", u=2)
+                src = turned[blocks][:, 0, :, :].rearrange("p u c -> p c u")
+            else:
+                dst = words.rearrange("p (k c u) -> p k c u", u=2, k=2)
+                src = turned[blocks][:].rearrange("p k u c -> p k c u")
+            if engine == SCALAR:
                 nc.scalar.copy(dst, src)
             else:
                 nc.vector.tensor_copy(dst, src)
-            hc = ring.tile([P, B], U32, name="hc", align_bytes=64)
-            hs = ring.tile([P, B], U8, name="hs", align_bytes=64)
-            nc.vector.quantize_mx(out=hc[:].bitcast(FP8), scales=hs[:], in_=hqw)
-            if (b // 4, 0) not in y:
-                for n in range(2):
-                    y[b // 4, n] = y_pool.tile([P, 4 * B], F32, name=f"y{n}")
-            at = m * 2 * B + (e % 2) * B
-            for n in range(2):
+
+        def quantise_h(e):
+            h_words[e] = ring.tile([P, C], U32, name="h_words", align_bytes=64)
+            h_bytes[e] = ring.tile([P, C], U8, name="h_bytes", align_bytes=64)
+            nc.vector.quantize_mx(
+                out=h_words[e][:].bitcast(E4M3),
+                scales=h_bytes[e][:],
+                in_=h_grouped[e][:].rearrange("p c d -> p (c d)"),
+            )
+
+        def layer2(e):
+            for g in range(2):
+                y[e, g] = y_pool.tile([P, C], F32, name=f"y{g}")
                 nc.tensor.matmul_mx(
-                    out=y[b // 4, n][:, at : at + B],
-                    lhsT=w2t[:, e, 256 * n : 256 * (n + 1)].bitcast(FP4),
-                    lhsT_scale=w2s[:, e, P * n : P * (n + 1)],
-                    rhs=hc[:].bitcast(FP8),
-                    rhs_scale=hs[:],
+                    out=y[e, g][:],
+                    lhsT=w2_codes[:, e, 2 * P * g : 2 * P * (g + 1)].bitcast(E2M1),
+                    lhsT_scale=w2_bytes[:, e, P * g : P * (g + 1)],
+                    rhs=h_words[e][:].bitcast(E4M3),
+                    rhs_scale=h_bytes[e][:],
                     start=True,
                     stop=True,
                 )
 
-        def store(g, engs):
-            for n in range(2):
-                o = ring.tile([P, 4 * B], F32, name=f"o{n}")
-                if engs[n] == "v":
-                    nc.vector.tensor_copy(o[:], y[g, n][:])
-                else:
-                    nc.scalar.copy(o[:], y[g, n][:])
-                dst = out[P * n : P * (n + 1), :].rearrange("n (m x) -> n m x", m=2)[:, :, 2 * B * g : 2 * B * (g + 1)]
-                nc.sync.dma_start(dst, o[:].rearrange("p (m x) -> p m x", m=2))
+        def store(e, g, engine):
+            result = ring.tile([P, C], F32, name=f"result{g}")
+            if engine == SCALAR:
+                nc.scalar.copy(result[:], y[e, g][:])
+            else:
+                nc.vector.tensor_copy(result[:], y[e, g][:])
+            columns = out[P * g : P * (g + 1), :].rearrange("n (m x) -> n m x", m=R)[:, :, P * e : P * (e + 1)]
+            nc.sync.dma_start(columns, result[:].rearrange("p (m x) -> p m x", m=R))
 
-        FULL_S = (("s", 0, H),)
-        FULL_V = (("v", 0, H),)
-        SQ = {"s": (("s", 0, P),), "v": (("v", 0, P),), "g": (("g", 0, P),)}
-        cast(0, "v", 0, 256)
-        cast(0, "s", 256, 512)
-        quant(0, 0, 512)
-        cast(0, "v", 512, 640)
-        cast(0, "s", 640, 768)
-        quant(0, 512, 768)
-        gather(gw[0], codes[0], 0, 512)
-        gather(gw[0], codes[0], 512, 1024)
-        cast(1, "v", 0, 256)
-        cast(1, "s", 256, 512)
-        quant(1, 0, 512)
-        cast(1, "v", 512, 640)
-        cast(1, "s", 640, 768)
-        quant(1, 512, 768)
-        gather(gb01, tsc01, 0, 512)
-        shift(0, 512)
-        cast(2, "v", 0, 256)
-        cast(2, "s", 256, 512)
-        cast(2, "s", 512, 640)
-        cast(2, "v", 640, 768)
-        gather(gw[1], codes[1], 0, 512)
-        for b in range(4):
+        load_tokens(0, 0, 512)
+        load_tokens(0, 512, T)
+        load_tokens(1, 0, T)
+        load_tokens(2, 0, T)
+        load_weight_scales()
+        load_w1(0)
+        load_w1(1)
+        load_w2()
+        load_w1(2)
+        load_w1(3)
+
+        for s in range(2):
+            cast(s, VECTOR, 0, 256)
+            cast(s, SCALAR, 256, 512)
+            cast(s, VECTOR, 512, 640)
+            cast(s, SCALAR, 640, T)
+            quantise_tokens(s)
+            if s == 0:
+                gather(slot_words[0], token_words[0], 0, SLOTS)
+        gather(slot_bytes01, token_bytes01, 0, SLOTS)
+        move_bytes1()
+
+        for a, b in ((0, 256), (256, 512), (512, 640), (640, T)):
+            cast(2, SCALAR, a, b)
+        gather(slot_words[1], token_words[1], 0, SLOTS)
+        for s in range(2):
+            for b in range(4):
+                layer1(b, s)
+        quantise_tokens(2)
+        gather(slot_bytes2, token_bytes2, 0, 512)
+
+        gather(slot_words[2], token_words[2], 0, 256)
+        layer1(0, 2)
+        layer1(1, 2)
+        gather(slot_words[2], token_words[2], 256, 512)
+        layer1(2, 2)
+        layer1(3, 2)
+        rectify(0, SCALAR)
+        rectify(1, SCALAR)
+        gather(slot_bytes2, token_bytes2, 512, SLOTS)
+        for b in (4, 5):
             layer1(b, 0)
-        for b in range(4):
             layer1(b, 1)
-        quant(2, 0, 512)
-        quant(2, 512, 768)
-        gather(gb2, tsc2, 0, 512)
-        gather(gw[2], codes[2], 0, 512)
-        for b in range(4):
-            layer1(b, 2)
-        gather(gb01, tsc01, 512, 1024)
-        shift(512, 1024)
-        relu_of(0, FULL_S)
-        relu_of(1, FULL_S)
-        square_of(0, SQ["s"])
-        gather(gw[1], codes[1], 512, 1024)
-        for b in range(4, 8):
-            layer1(b, 0)
-        relu_of(2, FULL_S)
-        square_of(1, SQ["s"])
-        gather(gb2, tsc2, 512, 1024)
-        second(0, "s")
-        relu_of(3, FULL_S)
-        square_of(2, SQ["s"])
-        second(1, "s")
-        for b in range(4, 8):
-            layer1(b, 1)
-        gather(gw[2], codes[2], 512, 1024)
-        for b in range(4, 8):
-            layer1(b, 2)
-        square_of(3, SQ["v"])
-        relu_of(4, FULL_S)
-        second(2, "s")
-        relu_of(5, FULL_V)
-        square_of(4, SQ["s"])
-        square_of(5, SQ["v"])
-        second(3, "v")
-        relu_of(6, FULL_S)
-        relu_of(7, FULL_V)
-        square_of(7, SQ["v"])
-        square_of(6, SQ["s"])
-        second(4, "s")
-        second(5, "v")
-        store(0, "sv")
-        second(7, "v")
-        second(6, "s")
-        store(1, "vs")
+        rectify(2, SCALAR)
+        square(0, SCALAR)
+        gather(slot_words[2], token_words[2], 512, 768)
+        layer1(4, 2)
+        layer1(5, 2)
+        rectify(3, SCALAR)
+        square(1, VECTOR)
+        turn(0, 1)
+        gather(slot_words[2], token_words[2], 768, SLOTS)
+        rectify(4, SCALAR)
+        for s in range(S):
+            layer1(6, s)
+        square(3, SCALAR)
+        square(2, VECTOR)
+        group(SCALAR, 0, 1)
+        turn(2, 3)
+        rectify(5, VECTOR)
+        for s in range(S):
+            layer1(7, s)
+        square(5, SCALAR)
+        quantise_h(0)
+        layer2(0)
+        square(4, VECTOR)
+        group(VECTOR, 2, 3)
+        turn(4, 5)
+        rectify(6, SCALAR)
+        store(0, 0, SCALAR)
+        rectify(7, SCALAR)
+        square(6, VECTOR)
+        quantise_h(1)
+        store(0, 1, SCALAR)
+        layer2(1)
+        group(SCALAR, 4, 5)
+        square(7, VECTOR)
+        store(1, 0, VECTOR)
+        store(1, 1, SCALAR)
+        turn(6)
+        turn(7)
+        quantise_h(2)
+        layer2(2)
+        group(SCALAR, 6)
+        group(VECTOR, 7)
+        store(2, 0, SCALAR)
+        store(2, 1, SCALAR)
+        quantise_h(3)
+        layer2(3)
+        store(3, 0, SCALAR)
+        store(3, 1, VECTOR)

from contextlib import ExitStack

import concourse.mybir as mybir
from concourse.masks import make_identity

F32 = mybir.dt.float32
BF16 = mybir.dt.bfloat16
I32 = mybir.dt.int32
U32 = mybir.dt.uint32
U16 = mybir.dt.uint16
U8 = mybir.dt.uint8
E4M3 = mybir.dt.float8_e4m3fn_x4
E2M1 = mybir.dt.float4_e2m1fn_x4
RELU = mybir.ActivationFunctionType.Relu
SQUARE = mybir.ActivationFunctionType.Square
MULT = mybir.AluOpType.mult
MAX = mybir.AluOpType.max

K, T, E, C, H, N = 1536, 768, 4, 256, 512, 256
R = 2
P = 128
S = K // 512
SLOTS = E * C
FLOPS = 2 * SLOTS * (K * H + H * N)

WIDE = 1536

VECTOR, SCALAR = "vector", "scalar"


def tile_moe_eps_mlp_relu2_kernel(tc, xT, w1_words, w1_scales, w2_words, w2_scales, offs, out):
    nc = tc.nc
    with ExitStack() as ctx:
        keep = ctx.enter_context(tc.tile_pool(name="keep", bufs=1))
        ring = ctx.enter_context(tc.tile_pool(name="ring", bufs=8))
        acc_pool = ctx.enter_context(tc.psum_pool(name="acc_pool", bufs=4))
        turn_pool = ctx.enter_context(tc.psum_pool(name="turn_pool", bufs=2))
        y_pool = ctx.enter_context(tc.psum_pool(name="y_pool", bufs=1))

        offsets = keep.tile([P, SLOTS // 16], U16, name="offsets")
        nc.sync.dma_start(offsets[:], offs)

        x_raw = [keep.tile([P, 4, T], F32, name=f"x_raw{s}") for s in range(S)]
        x_grouped = [keep.tile([P, T, 4], BF16, name=f"x_grouped{s}", align_bytes=64) for s in range(S)]
        w1_codes = [keep.tile([P, S, 2 * H], U8, name=f"w1_codes{e}", align_bytes=64) for e in range(E)]
        w1_bytes = keep.tile([P, E, S, H], U8, name="w1_bytes", align_bytes=64)
        w2_codes = keep.tile([P, E, 2 * N], U8, name="w2_codes", align_bytes=64)
        w2_bytes = keep.tile([P, E, N], U8, name="w2_bytes", align_bytes=64)

        token_words = [keep.tile([P, (WIDE, WIDE, T)[s]], U32, name=f"token_words{s}", align_bytes=64) for s in range(S)]
        token_bytes01 = keep.tile([P, WIDE], U8, name="token_bytes01", align_bytes=64)
        token_bytes2 = keep.tile([P, T], U8, name="token_bytes2", align_bytes=64)

        slot_words = [keep.tile([P, SLOTS], U32, name=f"slot_words{s}", align_bytes=64) for s in range(S)]
        slot_bytes01 = keep.tile([P, SLOTS], U8, name="slot_bytes01", align_bytes=64)
        slot_bytes1 = keep.tile([P, SLOTS], U8, name="slot_bytes1", align_bytes=64)
        slot_bytes2 = keep.tile([P, SLOTS], U8, name="slot_bytes2", align_bytes=64)
        slot_planes = (slot_bytes01, slot_bytes1, slot_bytes2)

        ident = keep.tile([P, P], F32, name="ident")
        first = keep.tile([P, 1], F32, name="first")

        nc.gpsimd.memset(first[:], 0.0)
        nc.vector.memset(token_bytes01[:].bitcast(I32), 0)
        nc.vector.memset(token_words[0][:, T:WIDE].bitcast(I32), 0)
        nc.vector.memset(token_words[1][:, T:WIDE].bitcast(I32), 0)
        nc.vector.memset(token_bytes2[:].bitcast(I32), 0)
        nc.gpsimd.memset(w1_bytes[:].rearrange("p e s n -> p (e s n)").bitcast(I32), 0)
        nc.gpsimd.memset(w2_bytes[:].rearrange("p e n -> p (e n)").bitcast(I32), 0)
        nc.gpsimd.memset(slot_bytes1[:].bitcast(I32), 0)
        make_identity(nc, ident[:])
        nc.scalar.activation(first[:], first[:], RELU)

        def load_tokens(s, a, b):
            rows = xT[512 * s : 512 * (s + 1), a:b].rearrange("(p j) w -> p j w", j=4)
            nc.sync.dma_start(x_raw[s][:, :, a:b], rows)

        def load_weight_scales():
            for q in range(4):
                nc.sync.dma_start(
                    w1_bytes[32 * q : 32 * q + 4, :, :, :].rearrange("p e s n -> p (e s) n").bitcast(I32),
                    w1_scales[:, :, 4 * q : 4 * q + 4, :].rearrange("e s q n -> q (e s) n").bitcast(I32),
                )
            for q in range(4):
                nc.sync.dma_start(
                    w2_bytes[32 * q : 32 * q + 4, :, :].bitcast(I32),
                    w2_scales[:, 0, 4 * q : 4 * q + 4, :].rearrange("e q n -> q e n").bitcast(I32),
                )

        def load_w1(e):
            nc.sync.dma_start(w1_codes[e][:].bitcast(I32), w1_words[e].rearrange("s p w -> p s w").bitcast(I32))

        def load_w2():
            nc.sync.dma_start(w2_codes[:].bitcast(I32), w2_words[:, 0].rearrange("e p w -> p e w").bitcast(I32))

        def cast(s, engine, a, b):
            dst = x_grouped[s][:, a:b, :].rearrange("p (c i) j -> p c j i", i=4)
            src = x_raw[s][:, :, a:b].rearrange("p j (c i) -> p c j i", i=4)
            if engine == VECTOR:
                nc.vector.tensor_copy(dst, src)
            else:
                nc.scalar.copy(dst, src)

        def quantise_tokens(s):
            plane, row = ((token_bytes01, 0), (token_bytes01, 4), (token_bytes2, 0))[s]
            for a, b in ((0, 512), (512, T)):
                nc.vector.quantize_mx(
                    out=token_words[s][:, a:b].bitcast(E4M3),
                    scales=plane[row:P, a:b],
                    in_=x_grouped[s][:, a:b, :].rearrange("p w j -> p (w j)"),
                )

        def gather(slots, tokens, a, b):
            nc.vector.tensor_copy(slots[:, a:b], tokens[:].indirect(offsets[:, a // 16 : b // 16]))

        def move_bytes1():
            for q in range(4):
                nc.sync.dma_start(
                    slot_bytes1[32 * q : 32 * q + 4, :].bitcast(I32),
                    slot_bytes01[32 * q + 4 : 32 * q + 8, :].bitcast(I32),
                )

        acc = {}

        def layer1(b, s):
            if s == 0:
                acc[b] = acc_pool.tile([P, H], F32, name="acc")
            slots = slice(P * b, P * (b + 1))
            nc.tensor.matmul_mx(
                out=acc[b][:],
                lhsT=slot_words[s][:, slots].bitcast(E4M3),
                lhsT_scale=slot_planes[s][:, slots],
                rhs=w1_codes[b // R][:, s, :].bitcast(E2M1),
                rhs_scale=w1_bytes[:, b // R, s, :],
                start=(s == 0),
                stop=(s == S - 1),
            )

        rectified = {}
        h = {}
        h_grouped = {}
        h_words = {}
        h_bytes = {}
        turned = {}
        y = {}

        def rectify(b, engine):
            rectified[b] = ring.tile([P, H], F32, name="rectified")
            if engine == SCALAR:
                nc.scalar.activation(rectified[b][:], acc[b][:], RELU)
            else:
                nc.vector.tensor_scalar(rectified[b][:], acc[b][:], 0.0, None, MAX)

        def square(b, engine):
            h[b] = ring.tile([P, 2, P, 2], BF16, name="h", align_bytes=64)
            v = rectified[b][:].rearrange("c (p u d) -> c u p d", u=2, d=2)
            if engine == SCALAR:
                nc.scalar.activation(h[b][:], v, SQUARE)
            else:
                nc.vector.tensor_tensor(h[b][:], v, v, MULT)

        def turn(*blocks):
            tile = turn_pool.tile([P, len(blocks), 2, P], F32, name="turned")
            for k, b in enumerate(blocks):
                words = h[b][:].rearrange("c u p d -> c (u p d)").bitcast(F32)
                for u in range(2):
                    nc.tensor.transpose(tile[:, k, u, :], words[:, P * u : P * (u + 1)], ident[:])
            turned[blocks] = tile

        def group(engine, *blocks):
            e = blocks[0] // R
            if e not in h_grouped:
                h_grouped[e] = ring.tile([P, C, 4], BF16, name="h_grouped", align_bytes=64)
            at = P * (blocks[0] % R)
            words = h_grouped[e][:, at : at + P * len(blocks), :].rearrange("p c d -> p (c d)").bitcast(F32)
            if len(blocks) == 1:
                dst = words.rearrange("p (c u) -> p c u", u=2)
                src = turned[blocks][:, 0, :, :].rearrange("p u c -> p c u")
            else:
                dst = words.rearrange("p (k c u) -> p k c u", u=2, k=2)
                src = turned[blocks][:].rearrange("p k u c -> p k c u")
            if engine == SCALAR:
                nc.scalar.copy(dst, src)
            else:
                nc.vector.tensor_copy(dst, src)

        def quantise_h(e):
            h_words[e] = ring.tile([P, C], U32, name="h_words", align_bytes=64)
            h_bytes[e] = ring.tile([P, C], U8, name="h_bytes", align_bytes=64)
            nc.vector.quantize_mx(
                out=h_words[e][:].bitcast(E4M3),
                scales=h_bytes[e][:],
                in_=h_grouped[e][:].rearrange("p c d -> p (c d)"),
            )

        def layer2(e):
            for g in range(2):
                y[e, g] = y_pool.tile([P, C], F32, name=f"y{g}")
                nc.tensor.matmul_mx(
                    out=y[e, g][:],
                    lhsT=w2_codes[:, e, 2 * P * g : 2 * P * (g + 1)].bitcast(E2M1),
                    lhsT_scale=w2_bytes[:, e, P * g : P * (g + 1)],
                    rhs=h_words[e][:].bitcast(E4M3),
                    rhs_scale=h_bytes[e][:],
                    start=True,
                    stop=True,
                )

        def store(e, g, engine):
            result = ring.tile([P, C], F32, name=f"result{g}")
            if engine == SCALAR:
                nc.scalar.copy(result[:], y[e, g][:])
            else:
                nc.vector.tensor_copy(result[:], y[e, g][:])
            columns = out[P * g : P * (g + 1), :].rearrange("n (m x) -> n m x", m=R)[:, :, P * e : P * (e + 1)]
            nc.sync.dma_start(columns, result[:].rearrange("p (m x) -> p m x", m=R))

        load_tokens(0, 0, 512)
        load_tokens(0, 512, T)
        load_tokens(1, 0, T)
        load_tokens(2, 0, T)
        load_weight_scales()
        load_w1(0)
        load_w1(1)
        load_w2()
        load_w1(2)
        load_w1(3)

        for s in range(2):
            cast(s, VECTOR, 0, 256)
            cast(s, SCALAR, 256, 512)
            cast(s, VECTOR, 512, 640)
            cast(s, SCALAR, 640, T)
            quantise_tokens(s)
            if s == 0:
                gather(slot_words[0], token_words[0], 0, SLOTS)
        gather(slot_bytes01, token_bytes01, 0, SLOTS)
        move_bytes1()

        for a, b in ((0, 256), (256, 512), (512, 640), (640, T)):
            cast(2, SCALAR, a, b)
        gather(slot_words[1], token_words[1], 0, SLOTS)
        for s in range(2):
            for b in range(4):
                layer1(b, s)
        quantise_tokens(2)
        gather(slot_bytes2, token_bytes2, 0, 512)

        gather(slot_words[2], token_words[2], 0, 256)
        layer1(0, 2)
        layer1(1, 2)
        gather(slot_words[2], token_words[2], 256, 512)
        layer1(2, 2)
        layer1(3, 2)
        rectify(0, SCALAR)
        rectify(1, SCALAR)
        gather(slot_bytes2, token_bytes2, 512, SLOTS)
        for b in (4, 5):
            layer1(b, 0)
            layer1(b, 1)
        rectify(2, SCALAR)
        square(0, SCALAR)
        gather(slot_words[2], token_words[2], 512, 768)
        layer1(4, 2)
        layer1(5, 2)
        rectify(3, SCALAR)
        square(1, VECTOR)
        turn(0, 1)
        gather(slot_words[2], token_words[2], 768, SLOTS)
        rectify(4, SCALAR)
        for s in range(S):
            layer1(6, s)
        square(3, SCALAR)
        square(2, VECTOR)
        group(SCALAR, 0, 1)
        turn(2, 3)
        rectify(5, VECTOR)
        for s in range(S):
            layer1(7, s)
        square(5, SCALAR)
        quantise_h(0)
        layer2(0)
        square(4, VECTOR)
        group(VECTOR, 2, 3)
        turn(4, 5)
        rectify(6, SCALAR)
        store(0, 0, SCALAR)
        rectify(7, SCALAR)
        square(6, VECTOR)
        quantise_h(1)
        store(0, 1, SCALAR)
        layer2(1)
        group(SCALAR, 4, 5)
        square(7, VECTOR)
        store(1, 0, VECTOR)
        store(1, 1, SCALAR)
        turn(6)
        turn(7)
        quantise_h(2)
        layer2(2)
        group(SCALAR, 6)
        group(VECTOR, 7)
        store(2, 0, SCALAR)
        store(2, 1, SCALAR)
        quantise_h(3)
        layer2(3)
        store(3, 0, SCALAR)
        store(3, 1, VECTOR)
